import numpy as np
import ml_dtypes


def mxq(x, axis, fmt="e4m3"):
    dtype, down = {"e4m3": (ml_dtypes.float8_e4m3fn, 7), "e5m2": (ml_dtypes.float8_e5m2, 14)}[fmt]
    v = np.moveaxis(np.asarray(x, np.float32).astype(ml_dtypes.bfloat16).astype(np.float64), axis, -1)
    blocks = v.reshape(v.shape[:-1] + (-1, 32))
    amax = np.abs(blocks).max(-1, keepdims=True)
    byte = np.maximum(np.where(amax > 0, np.frexp(amax)[1] - 1 + 127, 0) - down, 1)
    scale = np.exp2(byte - 127.0)
    codes = (blocks / scale).astype(np.float32).astype(dtype).astype(np.float64)
    return np.moveaxis((codes * scale).reshape(v.shape), -1, axis)


WIDE = False


def mx_kscale(k):
    if not WIDE:
        return np.ones(k)
    levels = np.array([10, -10, 5, -5, 0])
    if k % 512:
        return np.exp2(np.random.permutation(np.resize(levels, k // 32))).repeat(32)
    a = np.empty((k // 512, 16))
    for p in range(k // 512):
        a[p, :8] = np.random.permutation(np.resize(levels, 8))
        for g in range(8):
            far = levels[np.abs(levels - a[p, g]) >= 10]
            a[p, g + 8] = far[np.random.randint(len(far))]
    return np.exp2(a.ravel()).repeat(32)


def f64(x):
    return np.asarray(x).astype(np.float64)


def striped(idx):
    return np.tile(idx.reshape(-1, 16).T, (8, 1)).astype(np.uint16)


def unstriped(offs):
    return offs[:16].T.reshape(-1).astype(np.int64)


def striped8(idx):
    return np.concatenate([x.reshape(-1, 16).T for x in idx]).astype(np.uint16)


def runs(offs, k):
    lists = np.stack([offs[16 * r : 16 * r + 16].T.reshape(-1) for r in range(8)]).astype(np.int64)
    return lists[np.arange(k) % 512 // 64]


def pack_weight(w):
    k, n = w.shape
    w = f64(np.asarray(w, np.float32).astype(ml_dtypes.bfloat16)).reshape(k // 32, 32, n)
    amax = np.abs(w).max(1)
    byte = np.clip(np.where(amax > 0, np.frexp(amax)[1] - 1 + 127 - 7, 1), 1, 254)
    scaled = (w * np.exp2(127.0 - byte)[:, None, :]).reshape(k, n).astype(np.float32)
    words = np.ascontiguousarray(scaled.reshape(k // 512, 128, 4, n).transpose(0, 1, 3, 2)).astype(ml_dtypes.float8_e4m3fn).view(np.uint8)
    return words, np.ascontiguousarray(byte.astype(np.uint8).reshape(k // 512, 16, n))


def unpack_weight(words, scales):
    g, p, n, _ = words.shape
    vals = np.ascontiguousarray(words).view(ml_dtypes.float8_e4m3fn).astype(np.float64) * np.repeat(np.exp2(scales.astype(np.float64) - 127.0), 8, axis=1)[..., None]
    return vals.transpose(0, 1, 3, 2).reshape(g * 512, n)


E2M1 = np.array([0.0, 0.5, 1.0, 1.5, 2.0, 3.0, 4.0, 6.0, -0.0, -0.5, -1.0, -1.5, -2.0, -3.0, -4.0, -6.0])


def pack_fp4(w):
    k, n = w.shape
    w = f64(np.asarray(w, np.float32).astype(ml_dtypes.bfloat16)).reshape(k // 32, 32, n)
    amax = np.abs(w).max(1)
    mant, ex = np.frexp(amax / 6.0)
    byte = np.clip(np.where(amax > 0, np.where(mant > 0.5, ex, ex - 1) + 127, 1), 1, 254)
    scaled = (w * np.exp2(127.0 - byte)[:, None, :]).reshape(k, n).astype(np.float32)
    c = np.ascontiguousarray(scaled.reshape(k // 512, 128, 4, n).transpose(0, 1, 3, 2)).astype(ml_dtypes.float4_e2m1fn).view(np.uint8) & 0xF
    words = (c[..., 0::2] | (c[..., 1::2] << 4)).reshape(k // 512, 128, 2 * n)
    return np.ascontiguousarray(words), np.ascontiguousarray(byte.astype(np.uint8).reshape(k // 512, 16, n))


def unpack_fp4(words, scales):
    g, _, n = scales.shape
    words = np.ascontiguousarray(words).reshape(g, 128, n, 2)
    nib = np.empty((g, 128, n, 4), np.uint8)
    nib[..., 0::2] = words & 0xF
    nib[..., 1::2] = words >> 4
    vals = E2M1[nib] * np.repeat(np.exp2(scales.astype(np.float64) - 127.0), 8, axis=1)[..., None]
    return vals.transpose(0, 1, 3, 2).reshape(g * 512, n)


def planes(y):
    n, m = y.shape
    v = y.astype(np.float32).astype(ml_dtypes.bfloat16).astype(np.float64).reshape(n // 32, 32, m)
    top = np.abs(v).max(1)
    byte = np.clip(np.where(top > 0, np.frexp(top)[1] - 1 + 127 - 7, 1), 1, 254)
    codes = (v * np.exp2(127.0 - byte)[:, None, :]).reshape(n, m).astype(np.float32).astype(ml_dtypes.float8_e4m3fn).view(np.uint8)
    words = codes.reshape(n // 512, 128, 4, m).transpose(0, 1, 3, 2)
    return np.ascontiguousarray(words), np.ascontiguousarray(byte.astype(np.uint8).reshape(n // 512, 16, m))


K, T, S, H, C = 512, 2048, 512, 512, 512


def setup_inputs():
    n = np.random.standard_normal
    s = mx_kscale(K)[:, None]
    packed_xT = pack_weight(n((K, T)) * s)
    packed_w1 = pack_fp4(n((K, H)) / np.sqrt(K) / s)
    return {
        "x_words": packed_xT[0],
        "x_scales": packed_xT[1],
        "w1_words": packed_w1[0],
        "w1_scales": packed_w1[1],
        "gs": (np.random.uniform(0.5, 1.5, (K, 1)) / s).astype(np.float32),
        "offs": striped(np.random.permutation(T)[:S]),
        "n1": striped8(np.stack([np.random.permutation(S) for _ in range(8)])),
        "n2": striped8(np.stack([np.random.permutation(S) for _ in range(8)])),
        "ca": striped(np.random.permutation(T)[:C]),
        "cb": striped(np.random.permutation(T)[:C]),
        "n3": striped8(np.stack([np.random.permutation(S) for _ in range(8)])),
        "n4": striped8(np.stack([np.random.permutation(S) for _ in range(8)])),
    }


def reference(x_words, x_scales, w1_words, w1_scales, gs, offs, n1, n2, ca, cb, n3, n4):
    x_ca = unpack_weight(x_words, x_scales)[:, unstriped(ca)]
    xq = unpack_weight(x_words, x_scales)[:, unstriped(offs)]
    y = unpack_fp4(w1_words, w1_scales).T @ xq
    z = f64(gs) * (y[np.arange(H)[:, None], runs(n1, H)] + 0.75 * (y[np.arange(H)[:, None], runs(n2, H)]))
    zq = mxq(z, 0, "e4m3")
    a = 0.0625 * (x_ca.T @ zq)
    x_cb = unpack_weight(x_words, x_scales)[:, unstriped(cb)]
    b = 0.0625 * (x_cb.T @ zq)
    out_0 = np.maximum(a, b[np.arange(C)[:, None], runs(n4, C)]) - (np.minimum(a[np.arange(C)[:, None], runs(n3, C)], b))
    return (out_0,) + planes(out_0)

@@ -1,0 +1,223 @@
+from contextlib import ExitStack
+
+import concourse.mybir as mybir
+from concourse.masks import make_identity
+
+K, T, S = 512, 2048, 512
+FLOPS = 3 * 2 * 512 * 512 * 512
+
+F32 = mybir.dt.float32
+BF16 = mybir.dt.bfloat16
+I32 = mybir.dt.int32
+U32 = mybir.dt.uint32
+U16 = mybir.dt.uint16
+U8 = mybir.dt.uint8
+FP8X4 = mybir.dt.float8_e4m3fn_x4
+FP4X4 = mybir.dt.float4_e2m1fn_x4
+ALU = mybir.AluOpType
+COPY = mybir.ActivationFunctionType.Copy
+
+P = 128
+PACK = 4
+HALF = 256
+OUT_PIECES = ((0, 256), (256, 128), (384, 128))
+
+
+def tile_picked_ccmpmaxbsum_none_po_kernel(tc, x_words, x_scales, w1_words, w1_scales, gs, offs, n1, n2, ca, cb, n3, n4, out_0, out_1, out_2):
+    nc = tc.nc
+    with ExitStack() as ctx:
+        keep = ctx.enter_context(tc.tile_pool(name="keep", bufs=1))
+        psum = ctx.enter_context(tc.psum_pool(name="psum", bufs=1))
+
+        def sb(name, shape, dtype):
+            return keep.tile(shape, dtype, name=name, align_bytes=64)
+
+        def bank(b, shape):
+            return psum.tile(shape, F32, name="bank%d" % b)
+
+        def load_list(name, src):
+            t = sb(name, [P, S // 16], U16)
+            nc.sync.dma_start(t[:], src)
+            return t
+
+        def load_scale_rows(queue, name, src, width):
+            t = sb(name, [P, width], U8)
+            nc.vector.memset(t[:].bitcast(I32), 0)
+            for q in range(4):
+                queue.dma_start(t[32 * q : 32 * q + 4, :].bitcast(I32), src[0, 4 * q : 4 * q + 4, :].bitcast(I32))
+            return t
+
+        xs = load_scale_rows(nc.scalar, "xs", x_scales, T)
+        w1s = load_scale_rows(nc.gpsimd, "w1s", w1_scales, S)
+        gs_t = sb("gs_t", [P, PACK], F32)
+        nc.gpsimd.dma_start(gs_t[:], gs.rearrange("(p t) o -> p (t o)", t=PACK))
+        offs_t = load_list("offs_t", offs)
+        w1w = sb("w1w", [P, 2 * S], U8)
+        nc.sync.dma_start(w1w[:].bitcast(I32), w1_words[0].bitcast(I32))
+        ca_t = load_list("ca_t", ca)
+        n2_t = load_list("n2_t", n2)
+        n1_t = load_list("n1_t", n1)
+        xw = sb("xw", [P, T], I32)
+        nc.sync.dma_start(xw[:], x_words[0].rearrange("p n t -> p (n t)").bitcast(I32))
+        cb_t = load_list("cb_t", cb)
+        n3_t = load_list("n3_t", n3)
+        n4_t = load_list("n4_t", n4)
+
+        ident = sb("ident", [P, P], F32)
+        make_identity(nc, ident[:])
+
+        def gather_bytes(name, lst):
+            t = sb(name, [P, S], U8)
+            nc.vector.tensor_copy(t[:], xs[:].indirect(lst[:]))
+            return t
+
+        def deal_bytes(name, src):
+            t = sb(name, [P, S], U8)
+            nc.vector.tensor_copy(t[:].rearrange("p (t m) -> p m t", t=PACK), src[:].rearrange("p (m t) -> p m t", t=PACK))
+            return t
+
+        def gather_words_dealt(name, lst):
+            t = sb(name, [P, S], U32)
+            nc.vector.tensor_copy(t[:].rearrange("p (t m) -> p m t", t=PACK), xw[:].bitcast(U32).indirect(lst[:]))
+            return t
+
+        xq_s = gather_bytes("xq_s", offs_t)
+        w1d = sb("w1d", [P, 2 * S], U8)
+        nc.vector.tensor_copy(
+            w1d[:].rearrange("p (t m b) -> p m t b", t=PACK, b=2), w1w[:].rearrange("p (m t b) -> p m t b", t=PACK, b=2)
+        )
+        xq_w = sb("xq_w", [P, S], U32)
+        nc.vector.tensor_copy(xq_w[:], xw[:].bitcast(U32).indirect(offs_t[:]))
+        w1sd = deal_bytes("w1sd", w1s)
+
+        y = []
+        for t in range(PACK):
+            acc = bank(t, [P, S])
+            nc.tensor.matmul_mx(
+                out=acc[:],
+                lhsT=w1d[:, 2 * P * t : 2 * P * (t + 1)].bitcast(FP4X4),
+                lhsT_scale=w1sd[:, P * t : P * (t + 1)],
+                rhs=xq_w[:].bitcast(FP8X4),
+                rhs_scale=xq_s[:],
+                start=True,
+                stop=True,
+            )
+            yt = sb("y%d" % t, [P, S], F32)
+            nc.scalar.activation(yt[:], acc[:], COPY, scale=gs_t[:, t : t + 1])
+            y.append(yt)
+
+        xa_w = gather_words_dealt("w1s", ca_t)
+        xa_sr = gather_bytes("xa_sr", ca_t)
+        xa_s = deal_bytes("xa_s", xa_sr)
+
+        def interleave(copy, name, src, w):
+            dst = sb(name, [P, w, PACK], BF16)
+            copy(dst[:].rearrange("p (c i) t -> p c t i", i=4), src[:].rearrange("p t (c i) -> p c t i", i=4))
+            return dst
+
+        def entries(lst, c0, w):
+            return lst[:, c0 // 16 : (c0 + w) // 16]
+
+        def score(acc, words, scales, t, c0, w):
+            nc.tensor.matmul_mx(
+                out=acc,
+                lhsT=words[:, P * t : P * (t + 1)].bitcast(FP8X4),
+                lhsT_scale=scales[:, P * t : P * (t + 1)],
+                rhs=zq_w[:, c0 : c0 + w].bitcast(FP8X4),
+                rhs_scale=zq_s[:, c0 : c0 + w],
+                start=True,
+                stop=True,
+            )
+
+        na = [sb("na%d" % t, [P, S], F32) for t in range(PACK)]
+        pb = [sb("pb%d" % t, [P, S], F32) for t in range(PACK)]
+        zq_w = sb("zq_w", [P, S], U32)
+        zq_s = sb("zq_s", [P, S], U8)
+        for h in range(2):
+            c0, w = HALF * h, HALF
+            z = sb("z%d" % h, [P, PACK, w], F32)
+            for pair in range(2):
+                part = sb("zb0" if (h, pair) == (1, 1) else "part%d_%d" % (h, pair), [P, 2, w], F32)
+                for u in range(2):
+                    nc.vector.tensor_scalar(part[:, u, :], y[2 * pair + u][:].indirect(entries(n2_t, c0, w)), 0.75, 0.0, ALU.mult, ALU.add)
+                for u in range(2):
+                    t = 2 * pair + u
+                    nc.vector.tensor_tensor(z[:, t, :], y[t][:].indirect(entries(n1_t, c0, w)), part[:, u, :], ALU.add)
+            if h == 1:
+                xb_sr = gather_bytes("zb0", cb_t)
+                xb_s = deal_bytes("xb_s", xb_sr)
+            zb = interleave(nc.scalar.copy, "zb%d" % h, z, w)
+            nc.vector.quantize_mx(
+                out=zq_w[:, c0 : c0 + w].bitcast(FP8X4), scales=zq_s[:, c0 : c0 + w], in_=zb[:].rearrange("p c t -> p (c t)")
+            )
+            for t in range(PACK):
+                acc = bank(4 * (1 - h) + t, [P, w])
+                score(acc[:], xa_w, xa_s, t, c0, w)
+                nc.scalar.activation(na[t][:, c0 : c0 + w], acc[:], COPY, scale=-0.0625)
+        xb_w = gather_words_dealt("zb1", cb_t)
+        for t in range(PACK):
+            acc = bank(4 + t, [P, S])
+            score(acc[:], xb_w, xb_s, t, 0, S)
+            nc.scalar.activation(pb[t][:], acc[:], COPY, scale=0.0625)
+
+        negc = {}
+        for n, (h, pair) in enumerate(((0, 1), (1, 0), (1, 1))):
+            turned = bank(n % 2, [P, 4, P])
+            for u in range(2):
+                t = 2 * pair + u
+                for jb in range(2):
+                    cols = slice(HALF * h + P * jb, HALF * h + P * (jb + 1))
+                    nc.tensor.matmul(turned[:, 2 * u + jb, :], na[t][:, cols], ident[:], start=True, stop=False, is_transpose=True)
+                    nc.tensor.matmul(turned[:, 2 * u + jb, :], pb[t][:, cols], ident[:], start=False, stop=True, is_transpose=True)
+            turned_sb = sb("turned%d" % n, [P, 4, P], F32)
+            nc.scalar.copy(turned_sb[:], turned[:])
+            back = bank(2 + n, [P, 2, HALF])
+            for u in range(2):
+                for jb in range(2):
+                    nc.tensor.transpose(back[:, u, P * jb : P * (jb + 1)], turned_sb[:, 2 * u + jb, :], ident[:])
+            negc[(h, pair)] = back
+
+        oq_w = sb("oq_w", [P, S], U32)
+        oq_s = sb("oq_s", [P, S], U8)
+        out_rows = out_0.rearrange("(p t) j -> p t j", t=PACK)
+        out_words = out_1[0].rearrange("p n t -> p (n t)").bitcast(I32)
+        last = len(OUT_PIECES) - 1
+        for g, (c0, w) in enumerate(OUT_PIECES):
+            h, lo = divmod(c0, HALF)
+            cols = slice(c0, c0 + w)
+            res = sb("res%d" % g, [P, PACK, w], F32)
+            d1, d2, upper = [], [], []
+            for pair in range(2):
+                d1.append(sb("ob%d" % (g - 1) if (g > 0 and pair == 1) else "d1_%d" % pair, [P, 2, w], F32))
+                d2.append(sb("d2_%d" % pair, [P, 2, w], F32))
+                upper.append(sb("upper%d" % pair, [P, 2, w], F32))
+                if (g, pair) == (0, 0):
+                    early = sb("early", [P, 2, w], F32)
+                    for u in range(2):
+                        nc.vector.tensor_copy(early[:, u, :], na[u][:].indirect(entries(n3_t, c0, w)))
+                    for u in range(2):
+                        nc.vector.tensor_tensor(d1[0][:, u, :], pb[u][:].indirect(entries(n4_t, c0, w)), na[u][:, cols], ALU.add)
+                        nc.vector.scalar_tensor_tensor(d2[0][:, u, :], pb[u][:, cols], -1.0, early[:, u, :], ALU.mult, ALU.max)
+                    for u in range(2):
+                        nc.vector.scalar_tensor_tensor(upper[0][:, u, :], d1[0][:, u, :], 0.0, na[u][:, cols], ALU.max, ALU.subtract)
+                else:
+                    for u in range(2):
+                        t = 2 * pair + u
+                        nc.vector.tensor_tensor(d1[pair][:, u, :], pb[t][:].indirect(entries(n4_t, c0, w)), na[t][:, cols], ALU.add)
+                        nc.vector.tensor_tensor(d2[pair][:, u, :], na[t][:].indirect(entries(n3_t, c0, w)), pb[t][:, cols], ALU.add)
+            for pair in range(2):
+                if (g, pair) != (0, 0):
+                    nc.vector.scalar_tensor_tensor(upper[pair][:], d1[pair][:], 0.0, negc[(h, pair)][:, :, lo : lo + w], ALU.max, ALU.subtract)
+            for pair in range(2):
+                rows = res[:, 2 * pair : 2 * pair + 2, :]
+                if (g, pair) == (0, 0):
+                    nc.vector.tensor_tensor(rows, d2[0][:], upper[0][:], ALU.add)
+                else:
+                    nc.vector.scalar_tensor_tensor(rows, d2[pair][:], 0.0, upper[pair][:], ALU.max, ALU.add)
+            nc.sync.dma_start(out_rows[:, :, cols], res[:])
+            ob = interleave(nc.vector.tensor_copy if g == last else nc.scalar.copy, "ob%d" % g, res, w)
+            nc.vector.quantize_mx(out=oq_w[:, cols].bitcast(FP8X4), scales=oq_s[:, cols], in_=ob[:].rearrange("p c t -> p (c t)"))
+            nc.sync.dma_start(out_words[:, cols], oq_w[:, cols].bitcast(I32))
+        for q in range(4):
+            queue = nc.scalar if q % 2 else nc.sync
+            queue.dma_start(out_2[0, 4 * q : 4 * q + 4, :].bitcast(I32), oq_s[32 * q : 32 * q + 4, :].bitcast(I32))

@@ -16,6 +16,7 @@ FP8X4 = mybir.dt.float8_e4m3fn_x4
 FP4X4 = mybir.dt.float4_e2m1fn_x4
 ALU = mybir.AluOpType
 COPY = mybir.ActivationFunctionType.Copy
+RELU = mybir.ActivationFunctionType.Relu
 
 P = 128
 PACK = 4
@@ -40,28 +41,28 @@ def tile_picked_ccmpmaxbsum_none_po_kernel(tc, x_words, x_scales, w1_words, w1_s
             nc.sync.dma_start(t[:], src)
             return t
 
-        def load_scale_rows(queue, name, src, width):
+        def load_scale_rows(clear, queues, name, src, width):
             t = sb(name, [P, width], U8)
-            nc.vector.memset(t[:].bitcast(I32), 0)
+            clear.memset(t[:].bitcast(I32), 0)
             for q in range(4):
-                queue.dma_start(t[32 * q : 32 * q + 4, :].bitcast(I32), src[0, 4 * q : 4 * q + 4, :].bitcast(I32))
+                queues[q].dma_start(t[32 * q : 32 * q + 4, :].bitcast(I32), src[0, 4 * q : 4 * q + 4, :].bitcast(I32))
             return t
 
-        xs = load_scale_rows(nc.scalar, "xs", x_scales, T)
-        w1s = load_scale_rows(nc.gpsimd, "w1s", w1_scales, S)
-        gs_t = sb("gs_t", [P, PACK], F32)
-        nc.gpsimd.dma_start(gs_t[:], gs.rearrange("(p t) o -> p (t o)", t=PACK))
-        offs_t = load_list("offs_t", offs)
+        xw = sb("xw", [P, T], I32)
+        nc.scalar.dma_start(xw[:], x_words[0].rearrange("p n t -> p (n t)").bitcast(I32))
         w1w = sb("w1w", [P, 2 * S], U8)
         nc.sync.dma_start(w1w[:].bitcast(I32), w1_words[0].bitcast(I32))
+        offs_t = load_list("offs_t", offs)
         ca_t = load_list("ca_t", ca)
+        gs_t = sb("gs_t", [P, PACK], F32)
+        nc.sync.dma_start(gs_t[:], gs.rearrange("(p t) o -> p (t o)", t=PACK))
         n2_t = load_list("n2_t", n2)
         n1_t = load_list("n1_t", n1)
-        xw = sb("xw", [P, T], I32)
-        nc.sync.dma_start(xw[:], x_words[0].rearrange("p n t -> p (n t)").bitcast(I32))
         cb_t = load_list("cb_t", cb)
         n3_t = load_list("n3_t", n3)
         n4_t = load_list("n4_t", n4)
+        xs = load_scale_rows(nc.vector, [nc.scalar] * 4, "xs", x_scales, T)
+        w1s = load_scale_rows(nc.gpsimd, [nc.gpsimd] * 2 + [nc.scalar] * 2, "w1s", w1_scales, S)
 
         ident = sb("ident", [P, P], F32)
         make_identity(nc, ident[:])
@@ -73,7 +74,7 @@ def tile_picked_ccmpmaxbsum_none_po_kernel(tc, x_words, x_scales, w1_words, w1_s
 
         def deal_bytes(name, src):
             t = sb(name, [P, S], U8)
-            nc.vector.tensor_copy(t[:].rearrange("p (t m) -> p m t", t=PACK), src[:].rearrange("p (m t) -> p m t", t=PACK))
+            nc.vector.tensor_copy(t[:].rearrange("p (t m) -> p t m", t=PACK), src[:].rearrange("p (m t) -> p t m", t=PACK))
             return t
 
         def gather_words_dealt(name, lst):
@@ -84,9 +85,9 @@ def tile_picked_ccmpmaxbsum_none_po_kernel(tc, x_words, x_scales, w1_words, w1_s
         xq_s = gather_bytes("xq_s", offs_t)
         w1d = sb("w1d", [P, 2 * S], U8)
         nc.vector.tensor_copy(
-            w1d[:].rearrange("p (t m b) -> p m t b", t=PACK, b=2), w1w[:].rearrange("p (m t b) -> p m t b", t=PACK, b=2)
+            w1d[:].rearrange("p (t m b) -> p t m b", t=PACK, b=2), w1w[:].rearrange("p (m t b) -> p t m b", t=PACK, b=2)
         )
-        xq_w = sb("xq_w", [P, S], U32)
+        xq_w = sb("w1w", [P, S], U32)
         nc.vector.tensor_copy(xq_w[:], xw[:].bitcast(U32).indirect(offs_t[:]))
         w1sd = deal_bytes("w1sd", w1s)
 
@@ -107,7 +108,7 @@ def tile_picked_ccmpmaxbsum_none_po_kernel(tc, x_words, x_scales, w1_words, w1_s
             y.append(yt)
 
         xa_w = gather_words_dealt("w1s", ca_t)
-        xa_sr = gather_bytes("xa_sr", ca_t)
+        xa_sr = gather_bytes("xq_s", ca_t)
         xa_s = deal_bytes("xa_s", xa_sr)
 
         def interleave(copy, name, src, w):
@@ -160,64 +161,107 @@ def tile_picked_ccmpmaxbsum_none_po_kernel(tc, x_words, x_scales, w1_words, w1_s
             score(acc[:], xb_w, xb_s, t, 0, S)
             nc.scalar.activation(pb[t][:], acc[:], COPY, scale=0.0625)
 
-        negc = {}
-        for n, (h, pair) in enumerate(((0, 1), (1, 0), (1, 1))):
-            turned = bank(n % 2, [P, 4, P])
+        def turn(dst, src, start, stop):
+            nc.tensor.matmul(dst, src, ident[:], start=start, stop=stop, is_transpose=True)
+
+        def turned_difference(name, b, pair, c0):
+            acc = bank(b, [P, 2, 2, P])
             for u in range(2):
                 t = 2 * pair + u
                 for jb in range(2):
-                    cols = slice(HALF * h + P * jb, HALF * h + P * (jb + 1))
-                    nc.tensor.matmul(turned[:, 2 * u + jb, :], na[t][:, cols], ident[:], start=True, stop=False, is_transpose=True)
-                    nc.tensor.matmul(turned[:, 2 * u + jb, :], pb[t][:, cols], ident[:], start=False, stop=True, is_transpose=True)
-            turned_sb = sb("turned%d" % n, [P, 4, P], F32)
-            nc.scalar.copy(turned_sb[:], turned[:])
-            back = bank(2 + n, [P, 2, HALF])
+                    cols = slice(c0 + P * jb, c0 + P * (jb + 1))
+                    turn(acc[:, u, jb, :], na[t][:, cols], True, False)
+                    turn(acc[:, u, jb, :], pb[t][:, cols], False, True)
+            diff = sb(name, [P, 2, 2, P], F32)
+            nc.scalar.activation(diff[:], acc[:], COPY, scale=-1.0)
+            return diff
+
+        diff = {(0, 1): turned_difference("diff01", 0, 1, 0), (1, 0): turned_difference("diff10", 1, 0, HALF), (1, 1): turned_difference("diff11", 0, 1, HALF)}
+
+        def gather_pair(name, pair, c0, w):
+            d = sb(name, [P, 2, 2, w], F32)
+            cols = slice(c0, c0 + w)
             for u in range(2):
-                for jb in range(2):
-                    nc.tensor.transpose(back[:, u, P * jb : P * (jb + 1)], turned_sb[:, 2 * u + jb, :], ident[:])
-            negc[(h, pair)] = back
+                t = 2 * pair + u
+                nc.vector.tensor_tensor(d[:, 0, u, :], na[t][:].indirect(entries(n3_t, c0, w)), pb[t][:, cols], ALU.add)
+            for u in range(2):
+                t = 2 * pair + u
+                nc.vector.tensor_tensor(d[:, 1, u, :], pb[t][:].indirect(entries(n4_t, c0, w)), na[t][:, cols], ALU.add)
+            return d
+
+        def rest_on_tensor(name, b_turn, b_back, d, pair, c0, w):
+            h, lo = divmod(c0, HALF)
+            nb = w // P
+            acc = bank(b_turn, [P, 2, nb, P])
+            for u in range(2):
+                for jb in range(nb):
+                    turn(acc[:, u, jb, :], d[:, 0, u, P * jb : P * (jb + 1)], True, True)
+            gap = sb(name, [P, 2, nb, P], F32)
+            nc.scalar.activation(gap[:], acc[:], RELU)
+            back = bank(b_back, [P, 2, w])
+            for u in range(2):
+                for jb in range(nb):
+                    turn(back[:, u, P * jb : P * (jb + 1)], diff[(h, pair)][:, u, lo // P + jb, :], True, False)
+                    turn(back[:, u, P * jb : P * (jb + 1)], gap[:, u, jb, :], False, True)
+            return back
 
         oq_w = sb("oq_w", [P, S], U32)
         oq_s = sb("oq_s", [P, S], U8)
         out_rows = out_0.rearrange("(p t) j -> p t j", t=PACK)
         out_words = out_1[0].rearrange("p n t -> p (n t)").bitcast(I32)
-        last = len(OUT_PIECES) - 1
-        for g, (c0, w) in enumerate(OUT_PIECES):
-            h, lo = divmod(c0, HALF)
+
+        def finish_pair(res, d, rest, pair):
+            nc.vector.scalar_tensor_tensor(res[:, 2 * pair : 2 * pair + 2, :], d[:, 1, :, :], 0.0, rest, ALU.max, ALU.add)
+
+        def hand_out(copy, name, res, c0, w):
             cols = slice(c0, c0 + w)
-            res = sb("res%d" % g, [P, PACK, w], F32)
-            d1, d2, upper = [], [], []
-            for pair in range(2):
-                d1.append(sb("ob%d" % (g - 1) if (g > 0 and pair == 1) else "d1_%d" % pair, [P, 2, w], F32))
-                d2.append(sb("d2_%d" % pair, [P, 2, w], F32))
-                upper.append(sb("upper%d" % pair, [P, 2, w], F32))
-                if (g, pair) == (0, 0):
-                    early = sb("early", [P, 2, w], F32)
-                    for u in range(2):
-                        nc.vector.tensor_copy(early[:, u, :], na[u][:].indirect(entries(n3_t, c0, w)))
-                    for u in range(2):
-                        nc.vector.tensor_tensor(d1[0][:, u, :], pb[u][:].indirect(entries(n4_t, c0, w)), na[u][:, cols], ALU.add)
-                        nc.vector.scalar_tensor_tensor(d2[0][:, u, :], pb[u][:, cols], -1.0, early[:, u, :], ALU.mult, ALU.max)
-                    for u in range(2):
-                        nc.vector.scalar_tensor_tensor(upper[0][:, u, :], d1[0][:, u, :], 0.0, na[u][:, cols], ALU.max, ALU.subtract)
-                else:
-                    for u in range(2):
-                        t = 2 * pair + u
-                        nc.vector.tensor_tensor(d1[pair][:, u, :], pb[t][:].indirect(entries(n4_t, c0, w)), na[t][:, cols], ALU.add)
-                        nc.vector.tensor_tensor(d2[pair][:, u, :], na[t][:].indirect(entries(n3_t, c0, w)), pb[t][:, cols], ALU.add)
-            for pair in range(2):
-                if (g, pair) != (0, 0):
-                    nc.vector.scalar_tensor_tensor(upper[pair][:], d1[pair][:], 0.0, negc[(h, pair)][:, :, lo : lo + w], ALU.max, ALU.subtract)
-            for pair in range(2):
-                rows = res[:, 2 * pair : 2 * pair + 2, :]
-                if (g, pair) == (0, 0):
-                    nc.vector.tensor_tensor(rows, d2[0][:], upper[0][:], ALU.add)
-                else:
-                    nc.vector.scalar_tensor_tensor(rows, d2[pair][:], 0.0, upper[pair][:], ALU.max, ALU.add)
             nc.sync.dma_start(out_rows[:, :, cols], res[:])
-            ob = interleave(nc.vector.tensor_copy if g == last else nc.scalar.copy, "ob%d" % g, res, w)
+            ob = interleave(copy, name, res, w)
             nc.vector.quantize_mx(out=oq_w[:, cols].bitcast(FP8X4), scales=oq_s[:, cols], in_=ob[:].rearrange("p c t -> p (c t)"))
             nc.sync.dma_start(out_words[:, cols], oq_w[:, cols].bitcast(I32))
+
+        (c0, w0), (c1, w1), (c2, w2) = OUT_PIECES
+        res0 = sb("res0", [P, PACK, w0], F32)
+        res1 = sb("res1", [P, PACK, w1], F32)
+        res2 = sb("res2", [P, PACK, w2], F32)
+
+        cols = slice(c0, c0 + w0)
+        early = sb("early", [P, 2, w0], F32)
+        d00 = sb("d00", [P, 2, 2, w0], F32)
+        upper = sb("upper", [P, 2, w0], F32)
+        for u in range(2):
+            nc.vector.tensor_copy(early[:, u, :], na[u][:].indirect(entries(n3_t, c0, w0)))
+        for u in range(2):
+            nc.vector.tensor_tensor(d00[:, 1, u, :], pb[u][:].indirect(entries(n4_t, c0, w0)), na[u][:, cols], ALU.add)
+            nc.vector.scalar_tensor_tensor(d00[:, 0, u, :], pb[u][:, cols], -1.0, early[:, u, :], ALU.mult, ALU.max)
+        d01 = gather_pair("d01", 1, c0, w0)
+        rest01 = rest_on_tensor("gap01", 2, 4, d01, 1, c0, w0)
+        for u in range(2):
+            nc.vector.scalar_tensor_tensor(upper[:, u, :], d00[:, 1, u, :], 0.0, na[u][:, cols], ALU.max, ALU.subtract)
+        nc.vector.tensor_tensor(res0[:, 0:2, :], d00[:, 0, :, :], upper[:], ALU.add)
+
+        d10 = gather_pair("d00", 0, c1, w1)
+        rest10 = rest_on_tensor("gap10", 3, 5, d10, 0, c1, w1)
+        finish_pair(res0, d01, rest01[:], 1)
+        d11 = gather_pair("d01", 1, c1, w1)
+        rest11 = rest_on_tensor("gap11", 2, 6, d11, 1, c1, w1)
+        hand_out(nc.scalar.copy, "ob0", res0, c0, w0)
+
+        last_diff = bank(7, [P, PACK, w2])
+        for t in range(PACK):
+            turn(last_diff[:, t, :], diff[(1, t // 2)][:, t % 2, 1, :], True, True)
+        d20 = gather_pair("ob0", 0, c2, w2)
+        finish_pair(res1, d10, rest10[:], 0)
+        d21 = gather_pair("d00", 1, c2, w2)
+        finish_pair(res1, d11, rest11[:], 1)
+        hand_out(nc.scalar.copy, "ob1", res1, c1, w1)
+        rest2 = sb("d01", [P, PACK, w2], F32)
+        for pair, d in enumerate((d20, d21)):
+            rows = slice(2 * pair, 2 * pair + 2)
+            nc.vector.scalar_tensor_tensor(rest2[:, rows, :], d[:, 0, :, :], 0.0, last_diff[:, rows, :], ALU.max, ALU.add)
+        for pair, d in enumerate((d20, d21)):
+            finish_pair(res2, d, rest2[:, 2 * pair : 2 * pair + 2, :], pair)
+        hand_out(nc.vector.tensor_copy, "ob2", res2, c2, w2)
         for q in range(4):
             queue = nc.scalar if q % 2 else nc.sync
             queue.dma_start(out_2[0, 4 * q : 4 * q + 4, :].bitcast(I32), oq_s[32 * q : 32 * q + 4, :].bitcast(I32))

@@ -62,7 +62,7 @@ def tile_picked_ccmpmaxbsum_none_po_kernel(tc, x_words, x_scales, w1_words, w1_s
         n3_t = load_list("n3_t", n3)
         n4_t = load_list("n4_t", n4)
         xs = load_scale_rows(nc.vector, [nc.scalar] * 4, "xs", x_scales, T)
-        w1s = load_scale_rows(nc.gpsimd, [nc.gpsimd] * 2 + [nc.scalar] * 2, "w1s", w1_scales, S)
+        w1s = load_scale_rows(nc.vector, [nc.gpsimd] * 2 + [nc.scalar] * 2, "w1s", w1_scales, S)
 
         ident = sb("ident", [P, P], F32)
         make_identity(nc, ident[:])
@@ -82,13 +82,14 @@ def tile_picked_ccmpmaxbsum_none_po_kernel(tc, x_words, x_scales, w1_words, w1_s
             nc.vector.tensor_copy(t[:].rearrange("p (t m) -> p m t", t=PACK), xw[:].bitcast(U32).indirect(lst[:]))
             return t
 
-        xq_s = gather_bytes("xq_s", offs_t)
         w1d = sb("w1d", [P, 2 * S], U8)
         nc.vector.tensor_copy(
             w1d[:].rearrange("p (t m b) -> p t m b", t=PACK, b=2), w1w[:].rearrange("p (m t b) -> p t m b", t=PACK, b=2)
         )
         xq_w = sb("w1w", [P, S], U32)
         nc.vector.tensor_copy(xq_w[:], xw[:].bitcast(U32).indirect(offs_t[:]))
+        xa_w = gather_words_dealt("xa_w", ca_t)
+        xq_s = gather_bytes("xq_s", offs_t)
         w1sd = deal_bytes("w1sd", w1s)
 
         y = []
@@ -107,8 +108,7 @@ def tile_picked_ccmpmaxbsum_none_po_kernel(tc, x_words, x_scales, w1_words, w1_s
             nc.scalar.activation(yt[:], acc[:], COPY, scale=gs_t[:, t : t + 1])
             y.append(yt)
 
-        xa_w = gather_words_dealt("w1s", ca_t)
-        xa_sr = gather_bytes("xq_s", ca_t)
+        xa_sr = gather_bytes("w1s", ca_t)
         xa_s = deal_bytes("xa_s", xa_sr)
 
         def interleave(copy, name, src, w):
@@ -176,7 +176,7 @@ def tile_picked_ccmpmaxbsum_none_po_kernel(tc, x_words, x_scales, w1_words, w1_s
             nc.scalar.activation(diff[:], acc[:], COPY, scale=-1.0)
             return diff
 
-        diff = {(0, 1): turned_difference("diff01", 0, 1, 0), (1, 0): turned_difference("diff10", 1, 0, HALF), (1, 1): turned_difference("diff11", 0, 1, HALF)}
+        diff = {(0, 1): turned_difference("diff01", 0, 1, 0), (1, 0): turned_difference("diff10", 1, 0, HALF)}
 
         def gather_pair(name, pair, c0, w):
             d = sb(name, [P, 2, 2, w], F32)
@@ -236,12 +236,13 @@ def tile_picked_ccmpmaxbsum_none_po_kernel(tc, x_words, x_scales, w1_words, w1_s
             nc.vector.scalar_tensor_tensor(d00[:, 0, u, :], pb[u][:, cols], -1.0, early[:, u, :], ALU.mult, ALU.max)
         d01 = gather_pair("d01", 1, c0, w0)
         rest01 = rest_on_tensor("gap01", 2, 4, d01, 1, c0, w0)
+        diff[(1, 1)] = turned_difference("diff11", 2, 1, HALF)
         for u in range(2):
             nc.vector.scalar_tensor_tensor(upper[:, u, :], d00[:, 1, u, :], 0.0, na[u][:, cols], ALU.max, ALU.subtract)
         nc.vector.tensor_tensor(res0[:, 0:2, :], d00[:, 0, :, :], upper[:], ALU.add)
 
         d10 = gather_pair("d00", 0, c1, w1)
-        rest10 = rest_on_tensor("gap10", 3, 5, d10, 0, c1, w1)
+        rest10 = rest_on_tensor("gap10", 2, 5, d10, 0, c1, w1)
         finish_pair(res0, d01, rest01[:], 1)
         d11 = gather_pair("d01", 1, c1, w1)
         rest11 = rest_on_tensor("gap11", 2, 6, d11, 1, c1, w1)

@@ -21,7 +21,6 @@ RELU = mybir.ActivationFunctionType.Relu
 P = 128
 PACK = 4
 HALF = 256
-OUT_PIECES = ((0, 256), (256, 128), (384, 128))
 
 
 def tile_picked_ccmpmaxbsum_none_po_kernel(tc, x_words, x_scales, w1_words, w1_scales, gs, offs, n1, n2, ca, cb, n3, n4, out_0, out_1, out_2):
@@ -64,6 +63,13 @@ def tile_picked_ccmpmaxbsum_none_po_kernel(tc, x_words, x_scales, w1_words, w1_s
         xs = load_scale_rows(nc.vector, [nc.scalar] * 4, "xs", x_scales, T)
         w1s = load_scale_rows(nc.vector, [nc.gpsimd] * 2 + [nc.scalar] * 2, "w1s", w1_scales, S)
 
+        def window(name, clear):
+            t = sb(name, [P, 2 * S], F32)
+            clear.memset(t[:, S:], 0.0)
+            return t
+
+        na = [window("na%d" % t, nc.vector) for t in range(PACK)]
+        pb = [window("pb%d" % t, nc.vector if t == 0 else nc.gpsimd) for t in range(PACK)]
         ident = sb("ident", [P, P], F32)
         make_identity(nc, ident[:])
 
@@ -92,7 +98,7 @@ def tile_picked_ccmpmaxbsum_none_po_kernel(tc, x_words, x_scales, w1_words, w1_s
         xq_s = gather_bytes("xq_s", offs_t)
         w1sd = deal_bytes("w1sd", w1s)
 
-        y = []
+        y = na
         for t in range(PACK):
             acc = bank(t, [P, S])
             nc.tensor.matmul_mx(
@@ -104,165 +110,136 @@ def tile_picked_ccmpmaxbsum_none_po_kernel(tc, x_words, x_scales, w1_words, w1_s
                 start=True,
                 stop=True,
             )
-            yt = sb("y%d" % t, [P, S], F32)
-            nc.scalar.activation(yt[:], acc[:], COPY, scale=gs_t[:, t : t + 1])
-            y.append(yt)
+            nc.scalar.activation(y[t][:, :S], acc[:], COPY, scale=gs_t[:, t : t + 1])
 
         xa_sr = gather_bytes("w1s", ca_t)
         xa_s = deal_bytes("xa_s", xa_sr)
 
-        def interleave(copy, name, src, w):
-            dst = sb(name, [P, w, PACK], BF16)
-            copy(dst[:].rearrange("p (c i) t -> p c t i", i=4), src[:].rearrange("p t (c i) -> p c t i", i=4))
+        def interleave(copy, name, src, h):
+            dst = sb(name, [P, HALF, PACK], BF16)
+            copy(
+                dst[:].rearrange("p (c i) t -> p c t i", i=4),
+                src[:, :, HALF * h : HALF * (h + 1)].rearrange("p t (c i) -> p c t i", i=4),
+            )
             return dst
 
-        def entries(lst, c0, w):
-            return lst[:, c0 // 16 : (c0 + w) // 16]
+        def quantise(words, scales, src, h):
+            cols = slice(HALF * h, HALF * (h + 1))
+            nc.vector.quantize_mx(out=words[:, cols].bitcast(FP8X4), scales=scales[:, cols], in_=src[:].rearrange("p c t -> p (c t)"))
 
-        def score(acc, words, scales, t, c0, w):
+        def score(acc, words, scales, t, cols):
             nc.tensor.matmul_mx(
                 out=acc,
                 lhsT=words[:, P * t : P * (t + 1)].bitcast(FP8X4),
                 lhsT_scale=scales[:, P * t : P * (t + 1)],
-                rhs=zq_w[:, c0 : c0 + w].bitcast(FP8X4),
-                rhs_scale=zq_s[:, c0 : c0 + w],
+                rhs=zq_w[:, cols].bitcast(FP8X4),
+                rhs_scale=zq_s[:, cols],
                 start=True,
                 stop=True,
             )
 
-        na = [sb("na%d" % t, [P, S], F32) for t in range(PACK)]
-        pb = [sb("pb%d" % t, [P, S], F32) for t in range(PACK)]
+        part = sb("part", [P, PACK, S], F32)
+        z = sb("z", [P, PACK, S], F32)
+        for pair in range(2):
+            tiles = (2 * pair, 2 * pair + 1)
+            for t in tiles:
+                nc.vector.tensor_scalar(part[:, t, :], y[t][:].indirect(n2_t[:]), 0.75, 0.0, ALU.mult, ALU.add)
+            for c0, w in ((0, S),) if pair == 0 else ((0, HALF), (HALF, HALF)):
+                for t in tiles:
+                    nc.vector.tensor_tensor(
+                        z[:, t, c0 : c0 + w], y[t][:].indirect(n1_t[:, c0 // 16 : (c0 + w) // 16]), part[:, t, c0 : c0 + w], ALU.add
+                    )
+
         zq_w = sb("zq_w", [P, S], U32)
         zq_s = sb("zq_s", [P, S], U8)
         for h in range(2):
-            c0, w = HALF * h, HALF
-            z = sb("z%d" % h, [P, PACK, w], F32)
-            for pair in range(2):
-                part = sb("zb0" if (h, pair) == (1, 1) else "part%d_%d" % (h, pair), [P, 2, w], F32)
-                for u in range(2):
-                    nc.vector.tensor_scalar(part[:, u, :], y[2 * pair + u][:].indirect(entries(n2_t, c0, w)), 0.75, 0.0, ALU.mult, ALU.add)
-                for u in range(2):
-                    t = 2 * pair + u
-                    nc.vector.tensor_tensor(z[:, t, :], y[t][:].indirect(entries(n1_t, c0, w)), part[:, u, :], ALU.add)
-            if h == 1:
+            cols = slice(HALF * h, HALF * (h + 1))
+            zb = interleave(nc.scalar.copy, "zb%d" % h, z, h)
+            quantise(zq_w, zq_s, zb, h)
+            for t in range(PACK):
+                acc = bank(4 * (1 - h) + t, [P, HALF])
+                score(acc[:], xa_w, xa_s, t, cols)
+                nc.scalar.activation(na[t][:, cols], acc[:], COPY, scale=-0.0625)
+            if h == 0:
                 xb_sr = gather_bytes("zb0", cb_t)
                 xb_s = deal_bytes("xb_s", xb_sr)
-            zb = interleave(nc.scalar.copy, "zb%d" % h, z, w)
-            nc.vector.quantize_mx(
-                out=zq_w[:, c0 : c0 + w].bitcast(FP8X4), scales=zq_s[:, c0 : c0 + w], in_=zb[:].rearrange("p c t -> p (c t)")
-            )
-            for t in range(PACK):
-                acc = bank(4 * (1 - h) + t, [P, w])
-                score(acc[:], xa_w, xa_s, t, c0, w)
-                nc.scalar.activation(na[t][:, c0 : c0 + w], acc[:], COPY, scale=-0.0625)
         xb_w = gather_words_dealt("zb1", cb_t)
         for t in range(PACK):
             acc = bank(4 + t, [P, S])
-            score(acc[:], xb_w, xb_s, t, 0, S)
-            nc.scalar.activation(pb[t][:], acc[:], COPY, scale=0.0625)
+            score(acc[:], xb_w, xb_s, t, slice(0, S))
+            nc.scalar.activation(pb[t][:, :S], acc[:], COPY, scale=0.0625)
 
         def turn(dst, src, start, stop):
             nc.tensor.matmul(dst, src, ident[:], start=start, stop=stop, is_transpose=True)
 
-        def turned_difference(name, b, pair, c0):
-            acc = bank(b, [P, 2, 2, P])
-            for u in range(2):
-                t = 2 * pair + u
-                for jb in range(2):
-                    cols = slice(c0 + P * jb, c0 + P * (jb + 1))
-                    turn(acc[:, u, jb, :], na[t][:, cols], True, False)
-                    turn(acc[:, u, jb, :], pb[t][:, cols], False, True)
-            diff = sb(name, [P, 2, 2, P], F32)
-            nc.scalar.activation(diff[:], acc[:], COPY, scale=-1.0)
-            return diff
+        def turned(name, b, terms, func, scale):
+            acc = bank(b, [P, S])
+            for jb in range(S // P):
+                cols = slice(P * jb, P * (jb + 1))
+                for n, term in enumerate(terms):
+                    turn(acc[:, cols], term[:, cols], n == 0, n == len(terms) - 1)
+            dst = sb(name, [P, S], F32)
+            nc.scalar.activation(dst[:], acc[:], func, scale=scale)
+            return dst
 
-        diff = {(0, 1): turned_difference("diff01", 0, 1, 0), (1, 0): turned_difference("diff10", 1, 0, HALF)}
+        def turned_back(b, terms):
+            acc = bank(b, [P, S])
+            for jb in range(S // P):
+                cols = slice(P * jb, P * (jb + 1))
+                for n, term in enumerate(terms):
+                    turn(acc[:, cols], term[:, cols], n == 0, n == len(terms) - 1)
+            return acc
 
-        def gather_pair(name, pair, c0, w):
-            d = sb(name, [P, 2, 2, w], F32)
-            cols = slice(c0, c0 + w)
-            for u in range(2):
-                t = 2 * pair + u
-                nc.vector.tensor_tensor(d[:, 0, u, :], na[t][:].indirect(entries(n3_t, c0, w)), pb[t][:, cols], ALU.add)
-            for u in range(2):
-                t = 2 * pair + u
-                nc.vector.tensor_tensor(d[:, 1, u, :], pb[t][:].indirect(entries(n4_t, c0, w)), na[t][:, cols], ALU.add)
+        def gap_below(t):
+            d = sb("below%d" % t, [P, S], F32)
+            nc.vector.tensor_tensor(d[:], na[t][:].indirect(n3_t[:]), pb[t][:, :S], ALU.add)
             return d
 
-        def rest_on_tensor(name, b_turn, b_back, d, pair, c0, w):
-            h, lo = divmod(c0, HALF)
-            nb = w // P
-            acc = bank(b_turn, [P, 2, nb, P])
-            for u in range(2):
-                for jb in range(nb):
-                    turn(acc[:, u, jb, :], d[:, 0, u, P * jb : P * (jb + 1)], True, True)
-            gap = sb(name, [P, 2, nb, P], F32)
-            nc.scalar.activation(gap[:], acc[:], RELU)
-            back = bank(b_back, [P, 2, w])
-            for u in range(2):
-                for jb in range(nb):
-                    turn(back[:, u, P * jb : P * (jb + 1)], diff[(h, pair)][:, u, lo // P + jb, :], True, False)
-                    turn(back[:, u, P * jb : P * (jb + 1)], gap[:, u, jb, :], False, True)
-            return back
+        def gap_above(t):
+            d = sb("above%d" % t, [P, S], F32)
+            nc.vector.tensor_tensor(d[:], pb[t][:].indirect(n4_t[:]), na[t][:, :S], ALU.add)
+            return d
+
+        res = sb("res", [P, PACK, S], F32)
+        out_rows = out_0.rearrange("(p t) j -> p t j", t=PACK)
+
+        def finish(t, above, rest):
+            nc.vector.scalar_tensor_tensor(res[:, t, :], above[:], 0.0, rest[:], ALU.max, ALU.add)
+            nc.sync.dma_start(out_rows[:, t, :], res[:, t, :])
+
+        early = sb("early", [P, S], F32)
+        nc.vector.tensor_copy(early[:], na[0][:].indirect(n3_t[:]))
+        above0 = gap_above(0)
+        lower = sb("lower", [P, S], F32)
+        nc.vector.scalar_tensor_tensor(lower[:], pb[0][:, :S], -1.0, early[:], ALU.mult, ALU.max)
+        upper = sb("upper", [P, S], F32)
+        nc.vector.scalar_tensor_tensor(upper[:], above0[:], 0.0, na[0][:, :S], ALU.max, ALU.subtract)
+
+        diff = {t: turned("diff%d" % t, t - 1, [na[t], pb[t]], COPY, -1.0) for t in range(1, PACK)}
+        above, rest = {}, {}
+        for t in (1, 2):
+            below = gap_below(t)
+            if t == 1:
+                nc.vector.tensor_tensor(res[:, 0, :], lower[:], upper[:], ALU.add)
+                nc.sync.dma_start(out_rows[:, 0, :], res[:, 0, :])
+            rest[t] = turned_back(3 + t, [diff[t], turned("gap%d" % t, 3, [below], RELU, 1.0)])
+            above[t] = gap_above(t)
+        diff3 = turned_back(6, [diff[3]])
+        below3 = gap_below(3)
+        above[3] = gap_above(3)
+        rest[3] = sb("rest3", [P, S], F32)
+        nc.vector.scalar_tensor_tensor(rest[3][:], below3[:], 0.0, diff3[:], ALU.max, ALU.add)
+        for t in (1, 2, 3):
+            finish(t, above[t], rest[t])
 
         oq_w = sb("oq_w", [P, S], U32)
         oq_s = sb("oq_s", [P, S], U8)
-        out_rows = out_0.rearrange("(p t) j -> p t j", t=PACK)
         out_words = out_1[0].rearrange("p n t -> p (n t)").bitcast(I32)
-
-        def finish_pair(res, d, rest, pair):
-            nc.vector.scalar_tensor_tensor(res[:, 2 * pair : 2 * pair + 2, :], d[:, 1, :, :], 0.0, rest, ALU.max, ALU.add)
-
-        def hand_out(copy, name, res, c0, w):
-            cols = slice(c0, c0 + w)
-            nc.sync.dma_start(out_rows[:, :, cols], res[:])
-            ob = interleave(copy, name, res, w)
-            nc.vector.quantize_mx(out=oq_w[:, cols].bitcast(FP8X4), scales=oq_s[:, cols], in_=ob[:].rearrange("p c t -> p (c t)"))
-            nc.sync.dma_start(out_words[:, cols], oq_w[:, cols].bitcast(I32))
-
-        (c0, w0), (c1, w1), (c2, w2) = OUT_PIECES
-        res0 = sb("res0", [P, PACK, w0], F32)
-        res1 = sb("res1", [P, PACK, w1], F32)
-        res2 = sb("res2", [P, PACK, w2], F32)
-
-        cols = slice(c0, c0 + w0)
-        early = sb("early", [P, 2, w0], F32)
-        d00 = sb("d00", [P, 2, 2, w0], F32)
-        upper = sb("upper", [P, 2, w0], F32)
-        for u in range(2):
-            nc.vector.tensor_copy(early[:, u, :], na[u][:].indirect(entries(n3_t, c0, w0)))
-        for u in range(2):
-            nc.vector.tensor_tensor(d00[:, 1, u, :], pb[u][:].indirect(entries(n4_t, c0, w0)), na[u][:, cols], ALU.add)
-            nc.vector.scalar_tensor_tensor(d00[:, 0, u, :], pb[u][:, cols], -1.0, early[:, u, :], ALU.mult, ALU.max)
-        d01 = gather_pair("d01", 1, c0, w0)
-        rest01 = rest_on_tensor("gap01", 2, 4, d01, 1, c0, w0)
-        diff[(1, 1)] = turned_difference("diff11", 2, 1, HALF)
-        for u in range(2):
-            nc.vector.scalar_tensor_tensor(upper[:, u, :], d00[:, 1, u, :], 0.0, na[u][:, cols], ALU.max, ALU.subtract)
-        nc.vector.tensor_tensor(res0[:, 0:2, :], d00[:, 0, :, :], upper[:], ALU.add)
-
-        d10 = gather_pair("d00", 0, c1, w1)
-        rest10 = rest_on_tensor("gap10", 2, 5, d10, 0, c1, w1)
-        finish_pair(res0, d01, rest01[:], 1)
-        d11 = gather_pair("d01", 1, c1, w1)
-        rest11 = rest_on_tensor("gap11", 2, 6, d11, 1, c1, w1)
-        hand_out(nc.scalar.copy, "ob0", res0, c0, w0)
-
-        last_diff = bank(7, [P, PACK, w2])
-        for t in range(PACK):
-            turn(last_diff[:, t, :], diff[(1, t // 2)][:, t % 2, 1, :], True, True)
-        d20 = gather_pair("ob0", 0, c2, w2)
-        finish_pair(res1, d10, rest10[:], 0)
-        d21 = gather_pair("d00", 1, c2, w2)
-        finish_pair(res1, d11, rest11[:], 1)
-        hand_out(nc.scalar.copy, "ob1", res1, c1, w1)
-        rest2 = sb("d01", [P, PACK, w2], F32)
-        for pair, d in enumerate((d20, d21)):
-            rows = slice(2 * pair, 2 * pair + 2)
-            nc.vector.scalar_tensor_tensor(rest2[:, rows, :], d[:, 0, :, :], 0.0, last_diff[:, rows, :], ALU.max, ALU.add)
-        for pair, d in enumerate((d20, d21)):
-            finish_pair(res2, d, rest2[:, 2 * pair : 2 * pair + 2, :], pair)
-        hand_out(nc.vector.tensor_copy, "ob2", res2, c2, w2)
+        ob0 = interleave(nc.scalar.copy, "ob0", res, 0)
+        ob1 = interleave(nc.vector.tensor_copy, "ob1", res, 1)
+        for h, ob in ((1, ob1), (0, ob0)):
+            quantise(oq_w, oq_s, ob, h)
+            nc.sync.dma_start(out_words[:, HALF * h : HALF * (h + 1)], oq_w[:, HALF * h : HALF * (h + 1)].bitcast(I32))
         for q in range(4):
             queue = nc.scalar if q % 2 else nc.sync
             queue.dma_start(out_2[0, 4 * q : 4 * q + 4, :].bitcast(I32), oq_s[32 * q : 32 * q + 4, :].bitcast(I32))

from contextlib import ExitStack

import concourse.mybir as mybir
from concourse.masks import make_identity

K, T, S = 512, 2048, 512
FLOPS = 3 * 2 * 512 * 512 * 512

F32 = mybir.dt.float32
BF16 = mybir.dt.bfloat16
I32 = mybir.dt.int32
U32 = mybir.dt.uint32
U16 = mybir.dt.uint16
U8 = mybir.dt.uint8
FP8X4 = mybir.dt.float8_e4m3fn_x4
FP4X4 = mybir.dt.float4_e2m1fn_x4
ALU = mybir.AluOpType
COPY = mybir.ActivationFunctionType.Copy
RELU = mybir.ActivationFunctionType.Relu

P = 128
PACK = 4
HALF = 256


def tile_picked_ccmpmaxbsum_none_po_kernel(tc, x_words, x_scales, w1_words, w1_scales, gs, offs, n1, n2, ca, cb, n3, n4, out_0, out_1, out_2):
    nc = tc.nc
    with ExitStack() as ctx:
        keep = ctx.enter_context(tc.tile_pool(name="keep", bufs=1))
        psum = ctx.enter_context(tc.psum_pool(name="psum", bufs=1))

        def sb(name, shape, dtype):
            return keep.tile(shape, dtype, name=name, align_bytes=64)

        def bank(b, shape):
            return psum.tile(shape, F32, name="bank%d" % b)

        def load_list(name, src):
            t = sb(name, [P, S // 16], U16)
            nc.sync.dma_start(t[:], src)
            return t

        def load_scale_rows(clear, queues, name, src, width):
            t = sb(name, [P, width], U8)
            clear.memset(t[:].bitcast(I32), 0)
            for q in range(4):
                queues[q].dma_start(t[32 * q : 32 * q + 4, :].bitcast(I32), src[0, 4 * q : 4 * q + 4, :].bitcast(I32))
            return t

        xw = sb("xw", [P, T], I32)
        nc.scalar.dma_start(xw[:], x_words[0].rearrange("p n t -> p (n t)").bitcast(I32))
        w1w = sb("w1w", [P, 2 * S], U8)
        nc.sync.dma_start(w1w[:].bitcast(I32), w1_words[0].bitcast(I32))
        offs_t = load_list("offs_t", offs)
        ca_t = load_list("ca_t", ca)
        gs_t = sb("gs_t", [P, PACK], F32)
        nc.sync.dma_start(gs_t[:], gs.rearrange("(p t) o -> p (t o)", t=PACK))
        n2_t = load_list("n2_t", n2)
        n1_t = load_list("n1_t", n1)
        cb_t = load_list("cb_t", cb)
        n3_t = load_list("n3_t", n3)
        n4_t = load_list("n4_t", n4)
        xs = load_scale_rows(nc.vector, [nc.scalar] * 4, "xs", x_scales, T)
        w1s = load_scale_rows(nc.vector, [nc.gpsimd] * 2 + [nc.scalar] * 2, "w1s", w1_scales, S)

        def window(name, clear):
            t = sb(name, [P, 2 * S], F32)
            clear.memset(t[:, S:], 0.0)
            return t

        na = [window("na%d" % t, nc.vector) for t in range(PACK)]
        pb = [window("pb%d" % t, nc.vector if t == 0 else nc.gpsimd) for t in range(PACK)]
        ident = sb("ident", [P, P], F32)
        make_identity(nc, ident[:])

        def gather_bytes(name, lst):
            t = sb(name, [P, S], U8)
            nc.vector.tensor_copy(t[:], xs[:].indirect(lst[:]))
            return t

        def deal_bytes(name, src):
            t = sb(name, [P, S], U8)
            nc.vector.tensor_copy(t[:].rearrange("p (t m) -> p t m", t=PACK), src[:].rearrange("p (m t) -> p t m", t=PACK))
            return t

        def gather_words_dealt(name, lst):
            t = sb(name, [P, S], U32)
            nc.vector.tensor_copy(t[:].rearrange("p (t m) -> p m t", t=PACK), xw[:].bitcast(U32).indirect(lst[:]))
            return t

        w1d = sb("w1d", [P, 2 * S], U8)
        nc.vector.tensor_copy(
            w1d[:].rearrange("p (t m b) -> p t m b", t=PACK, b=2), w1w[:].rearrange("p (m t b) -> p t m b", t=PACK, b=2)
        )
        xq_w = sb("w1w", [P, S], U32)
        nc.vector.tensor_copy(xq_w[:], xw[:].bitcast(U32).indirect(offs_t[:]))
        xa_w = gather_words_dealt("xa_w", ca_t)
        xq_s = gather_bytes("xq_s", offs_t)
        w1sd = deal_bytes("w1sd", w1s)

        y = na
        for t in range(PACK):
            acc = bank(t, [P, S])
            nc.tensor.matmul_mx(
                out=acc[:],
                lhsT=w1d[:, 2 * P * t : 2 * P * (t + 1)].bitcast(FP4X4),
                lhsT_scale=w1sd[:, P * t : P * (t + 1)],
                rhs=xq_w[:].bitcast(FP8X4),
                rhs_scale=xq_s[:],
                start=True,
                stop=True,
            )
            nc.scalar.activation(y[t][:, :S], acc[:], COPY, scale=gs_t[:, t : t + 1])

        xa_sr = gather_bytes("w1s", ca_t)
        xa_s = deal_bytes("xa_s", xa_sr)

        def interleave(copy, name, src, h):
            dst = sb(name, [P, HALF, PACK], BF16)
            copy(
                dst[:].rearrange("p (c i) t -> p c t i", i=4),
                src[:, :, HALF * h : HALF * (h + 1)].rearrange("p t (c i) -> p c t i", i=4),
            )
            return dst

        def quantise(words, scales, src, h):
            cols = slice(HALF * h, HALF * (h + 1))
            nc.vector.quantize_mx(out=words[:, cols].bitcast(FP8X4), scales=scales[:, cols], in_=src[:].rearrange("p c t -> p (c t)"))

        def score(acc, words, scales, t, cols):
            nc.tensor.matmul_mx(
                out=acc,
                lhsT=words[:, P * t : P * (t + 1)].bitcast(FP8X4),
                lhsT_scale=scales[:, P * t : P * (t + 1)],
                rhs=zq_w[:, cols].bitcast(FP8X4),
                rhs_scale=zq_s[:, cols],
                start=True,
                stop=True,
            )

        part = sb("part", [P, PACK, S], F32)
        z = sb("z", [P, PACK, S], F32)
        for pair in range(2):
            tiles = (2 * pair, 2 * pair + 1)
            for t in tiles:
                nc.vector.tensor_scalar(part[:, t, :], y[t][:].indirect(n2_t[:]), 0.75, 0.0, ALU.mult, ALU.add)
            for c0, w in ((0, S),) if pair == 0 else ((0, HALF), (HALF, HALF)):
                for t in tiles:
                    nc.vector.tensor_tensor(
                        z[:, t, c0 : c0 + w], y[t][:].indirect(n1_t[:, c0 // 16 : (c0 + w) // 16]), part[:, t, c0 : c0 + w], ALU.add
                    )

        zq_w = sb("zq_w", [P, S], U32)
        zq_s = sb("zq_s", [P, S], U8)
        for h in range(2):
            cols = slice(HALF * h, HALF * (h + 1))
            zb = interleave(nc.scalar.copy, "zb%d" % h, z, h)
            quantise(zq_w, zq_s, zb, h)
            for t in range(PACK):
                acc = bank(4 * (1 - h) + t, [P, HALF])
                score(acc[:], xa_w, xa_s, t, cols)
                nc.scalar.activation(na[t][:, cols], acc[:], COPY, scale=-0.0625)
            if h == 0:
                xb_sr = gather_bytes("zb0", cb_t)
                xb_s = deal_bytes("xb_s", xb_sr)
        xb_w = gather_words_dealt("zb1", cb_t)
        for t in range(PACK):
            acc = bank(4 + t, [P, S])
            score(acc[:], xb_w, xb_s, t, slice(0, S))
            nc.scalar.activation(pb[t][:, :S], acc[:], COPY, scale=0.0625)

        def turn(dst, src, start, stop):
            nc.tensor.matmul(dst, src, ident[:], start=start, stop=stop, is_transpose=True)

        def turned(name, b, terms, func, scale):
            acc = bank(b, [P, S])
            for jb in range(S // P):
                cols = slice(P * jb, P * (jb + 1))
                for n, term in enumerate(terms):
                    turn(acc[:, cols], term[:, cols], n == 0, n == len(terms) - 1)
            dst = sb(name, [P, S], F32)
            nc.scalar.activation(dst[:], acc[:], func, scale=scale)
            return dst

        def turned_back(b, terms):
            acc = bank(b, [P, S])
            for jb in range(S // P):
                cols = slice(P * jb, P * (jb + 1))
                for n, term in enumerate(terms):
                    turn(acc[:, cols], term[:, cols], n == 0, n == len(terms) - 1)
            return acc

        def gap_below(t):
            d = sb("below%d" % t, [P, S], F32)
            nc.vector.tensor_tensor(d[:], na[t][:].indirect(n3_t[:]), pb[t][:, :S], ALU.add)
            return d

        def gap_above(t):
            d = sb("above%d" % t, [P, S], F32)
            nc.vector.tensor_tensor(d[:], pb[t][:].indirect(n4_t[:]), na[t][:, :S], ALU.add)
            return d

        res = sb("res", [P, PACK, S], F32)
        out_rows = out_0.rearrange("(p t) j -> p t j", t=PACK)

        def finish(t, above, rest):
            nc.vector.scalar_tensor_tensor(res[:, t, :], above[:], 0.0, rest[:], ALU.max, ALU.add)
            nc.sync.dma_start(out_rows[:, t, :], res[:, t, :])

        early = sb("early", [P, S], F32)
        nc.vector.tensor_copy(early[:], na[0][:].indirect(n3_t[:]))
        above0 = gap_above(0)
        lower = sb("lower", [P, S], F32)
        nc.vector.scalar_tensor_tensor(lower[:], pb[0][:, :S], -1.0, early[:], ALU.mult, ALU.max)
        upper = sb("upper", [P, S], F32)
        nc.vector.scalar_tensor_tensor(upper[:], above0[:], 0.0, na[0][:, :S], ALU.max, ALU.subtract)

        diff = {t: turned("diff%d" % t, t - 1, [na[t], pb[t]], COPY, -1.0) for t in range(1, PACK)}
        above, rest = {}, {}
        for t in (1, 2):
            below = gap_below(t)
            if t == 1:
                nc.vector.tensor_tensor(res[:, 0, :], lower[:], upper[:], ALU.add)
                nc.sync.dma_start(out_rows[:, 0, :], res[:, 0, :])
            rest[t] = turned_back(3 + t, [diff[t], turned("gap%d" % t, 3, [below], RELU, 1.0)])
            above[t] = gap_above(t)
        diff3 = turned_back(6, [diff[3]])
        below3 = gap_below(3)
        above[3] = gap_above(3)
        rest[3] = sb("rest3", [P, S], F32)
        nc.vector.scalar_tensor_tensor(rest[3][:], below3[:], 0.0, diff3[:], ALU.max, ALU.add)
        for t in (1, 2, 3):
            finish(t, above[t], rest[t])

        oq_w = sb("oq_w", [P, S], U32)
        oq_s = sb("oq_s", [P, S], U8)
        out_words = out_1[0].rearrange("p n t -> p (n t)").bitcast(I32)
        ob0 = interleave(nc.scalar.copy, "ob0", res, 0)
        ob1 = interleave(nc.vector.tensor_copy, "ob1", res, 1)
        for h, ob in ((1, ob1), (0, ob0)):
            quantise(oq_w, oq_s, ob, h)
            nc.sync.dma_start(out_words[:, HALF * h : HALF * (h + 1)], oq_w[:, HALF * h : HALF * (h + 1)].bitcast(I32))
        for q in range(4):
            queue = nc.scalar if q % 2 else nc.sync
            queue.dma_start(out_2[0, 4 * q : 4 * q + 4, :].bitcast(I32), oq_s[32 * q : 32 * q + 4, :].bitcast(I32))
